import numpy as np
import ml_dtypes


def mxq(x, axis, fmt="e4m3"):
    dtype, down = {"e4m3": (ml_dtypes.float8_e4m3fn, 7), "e5m2": (ml_dtypes.float8_e5m2, 14)}[fmt]
    v = np.moveaxis(np.asarray(x, np.float32).astype(ml_dtypes.bfloat16).astype(np.float64), axis, -1)
    blocks = v.reshape(v.shape[:-1] + (-1, 32))
    amax = np.abs(blocks).max(-1, keepdims=True)
    byte = np.maximum(np.where(amax > 0, np.frexp(amax)[1] - 1 + 127, 0) - down, 1)
    scale = np.exp2(byte - 127.0)
    codes = (blocks / scale).astype(np.float32).astype(dtype).astype(np.float64)
    return np.moveaxis((codes * scale).reshape(v.shape), -1, axis)


WIDE = False


def mx_kscale(k):
    if not WIDE:
        return np.ones(k)
    levels = np.array([10, -10, 5, -5, 0])
    if k % 512:
        return np.exp2(np.random.permutation(np.resize(levels, k // 32))).repeat(32)
    a = np.empty((k // 512, 16))
    for p in range(k // 512):
        a[p, :8] = np.random.permutation(np.resize(levels, 8))
        for g in range(8):
            far = levels[np.abs(levels - a[p, g]) >= 10]
            a[p, g + 8] = far[np.random.randint(len(far))]
    return np.exp2(a.ravel()).repeat(32)


def f64(x):
    return np.asarray(x).astype(np.float64)


def striped(idx):
    return np.tile(np.asarray(idx).reshape(-1, 16).T, (8, 1)).astype(np.uint16)


def unstriped(offs):
    return offs[:16].T.reshape(-1).astype(np.int64)


E2M1 = np.array([0.0, 0.5, 1.0, 1.5, 2.0, 3.0, 4.0, 6.0, -0.0, -0.5, -1.0, -1.5, -2.0, -3.0, -4.0, -6.0])


def pack_weight(w, fmt):
    k, n = w.shape
    w = f64(np.asarray(w, np.float32).astype(ml_dtypes.bfloat16)).reshape(k // 32, 32, n)
    amax = np.abs(w).max(1)
    if fmt == "e4m3":
        byte = np.frexp(amax)[1] - 1 + 127 - 7
    else:
        mant, ex = np.frexp(amax / 6.0)
        byte = np.where(mant > 0.5, ex, ex - 1) + 127
    byte = np.clip(np.where(amax > 0, byte, 1), 1, 254)
    scaled = (w * np.exp2(127.0 - byte)[:, None, :]).reshape(k, n).astype(np.float32)
    by_word = np.ascontiguousarray(scaled.reshape(k // 512, 128, 4, n).transpose(0, 1, 3, 2))
    if fmt == "e4m3":
        words = by_word.astype(ml_dtypes.float8_e4m3fn).view(np.uint8)
    else:
        c = by_word.astype(ml_dtypes.float4_e2m1fn).view(np.uint8) & 0xF
        words = (c[..., 0::2] | (c[..., 1::2] << 4)).reshape(k // 512, 128, 2 * n)
    return np.ascontiguousarray(words), np.ascontiguousarray(byte.astype(np.uint8).reshape(k // 512, 16, n))


def unpack_weight(words, scales, fmt):
    g, _, n = scales.shape
    words = np.ascontiguousarray(words).reshape(g, 128, n, -1)
    if fmt == "e4m3":
        vals = words.view(ml_dtypes.float8_e4m3fn).astype(np.float64)
    else:
        nib = np.empty((g, 128, n, 4), np.uint8)
        nib[..., 0::2] = words & 0xF
        nib[..., 1::2] = words >> 4
        vals = E2M1[nib]
    vals = vals * np.repeat(np.exp2(scales.astype(np.float64) - 127.0), 8, axis=1)[..., None]
    return vals.transpose(0, 1, 3, 2).reshape(g * 512, n)


D, T, I, Q, E, U = 512, 2048, 512, 128, 512, 512


def setup_inputs():
    n = np.random.standard_normal
    idx = np.random.permutation(T)[:I]
    idx2 = np.random.randint(0, U, I)
    fd = mx_kscale(D)
    fi = mx_kscale(I)
    ti = np.ones(T)
    ti[idx] = fi
    keysp = pack_weight(n((D, T)) / fd[:, None], "e4m3")
    return {
        "query": (n((D, Q)) * 0.25 / np.sqrt(D) * fd[:, None]).astype(np.float32),
        "keys_words": keysp[0],
        "keys_scales": keysp[1],
        "pquery": (n((D, Q)) * 1.0 / np.sqrt(D) * fd[:, None]).astype(np.float32),
        "place": (n((D, U)) / fd[:, None]).astype(np.float32),
        "size": (np.random.uniform(0.5, 2.0, (1, I)) * fi).astype(np.float32),
        "vals": (n((E, T)) / ti).astype(np.float32),
        "offs": striped(idx),
        "offs2": striped(idx2),
    }


def reference(query, keys_words, keys_scales, pquery, place, size, vals, offs, offs2):
    idx = unstriped(offs)
    idx2 = unstriped(offs2)
    keysu = unpack_weight(keys_words, keys_scales, "e4m3")
    queryq = mxq(f64(query), 0, "e4m3")
    keysidxg = keysu[:, idx]
    a = queryq.T @ keysidxg
    pqueryq = mxq(f64(pquery), 0, "e4m3")
    placeq = mxq(f64(place), 0, "e4m3")
    b = pqueryq.T @ placeq
    s = a * (b[:, idx2] + 1.0)
    p = np.exp(s - np.max(s, axis=1, keepdims=True))
    w = p * f64(size) / np.sum(p, axis=1, keepdims=True)
    wt = w.T
    vt = f64(vals)[:, idx].T
    wtq = mxq(wt, 0, "e4m3")
    vtq = mxq(vt, 0, "e4m3")
    o = wtq.T @ vtq
    return o

@@ -1,0 +1,169 @@
+from contextlib import ExitStack
+
+import concourse.mybir as mybir
+from concourse.masks import make_identity
+
+D, T, I, Q, E, U = 512, 2048, 512, 128, 512, 512
+FLOPS = 2 * Q * D * I + 2 * Q * D * U + 2 * Q * I * E
+
+F32 = mybir.dt.float32
+BF16 = mybir.dt.bfloat16
+I32 = mybir.dt.int32
+U32 = mybir.dt.uint32
+U16 = mybir.dt.uint16
+U8 = mybir.dt.uint8
+FP8X4 = mybir.dt.float8_e4m3fn_x4
+ALU = mybir.AluOpType
+ACT = mybir.ActivationFunctionType
+
+P = 128
+PACK = 4
+B_WINDOW = U + 192
+PLACE_ON_VECTOR = 320
+
+
+def interleave(copy, grouped, raw, c0, c1):
+    copy(
+        out=grouped[:, c0:c1, :].rearrange("p (c i) t -> p c t i", i=4),
+        in_=raw[:, :, c0:c1].rearrange("p t (c i) -> p c t i", i=4),
+    )
+
+
+def quantize(nc, pool, grouped, width, name):
+    codes = pool.tile([P, width], U32, name=name + "_codes", align_bytes=64)
+    scales = pool.tile([P, width], U8, name=name + "_scales", align_bytes=64)
+    nc.vector.quantize_mx(out=codes[:].bitcast(FP8X4), scales=scales[:], in_=grouped)
+    return codes, scales
+
+
+def tile_attend_productscores_kernel(tc, query, keys_words, keys_scales, pquery, place, size, vals, offs, offs2, out):
+    nc = tc.nc
+    with ExitStack() as ctx:
+        sb = ctx.enter_context(tc.tile_pool(name="sb", bufs=1))
+        ps = ctx.enter_context(tc.psum_pool(name="ps", bufs=1))
+        ps2 = ctx.enter_context(tc.psum_pool(name="ps2", bufs=2))
+
+        slots = sb.tile([P, I // 16], U16, name="slots")
+        places = sb.tile([P, I // 16], U16, name="places")
+        key_scale_pool = sb.tile([P, T], U8, name="key_scale_pool", align_bytes=64)
+        key_word_pool = sb.tile([P, T], I32, name="key_word_pool", align_bytes=64)
+        q_raw = sb.tile([P, PACK, Q], F32, name="q_raw")
+        pq_raw = sb.tile([P, PACK, Q], F32, name="pq_raw")
+        place_raw = sb.tile([P, PACK, U], F32, name="place_raw")
+        size_cols = sb.tile([P, PACK], F32, name="size_cols")
+        val_pool = [sb.tile([P, T], F32, name="val_pool%d" % j) for j in range(E // P)]
+        b_sb = sb.tile([P, B_WINDOW], F32, name="b_sb")
+
+        nc.vector.memset(key_scale_pool[:].bitcast(I32), 0)
+        nc.vector.memset(b_sb[:, U:], 0.0)
+        nc.sync.dma_start(slots[:], offs)
+        for g in range(4):
+            nc.scalar.dma_start(
+                key_scale_pool[32 * g : 32 * g + 4, :].bitcast(I32), keys_scales[0, 4 * g : 4 * g + 4, :].bitcast(I32)
+            )
+        nc.sync.dma_start(pq_raw[:], pquery.rearrange("(p t) q -> p t q", t=PACK))
+        nc.sync.dma_start(place_raw[:], place.rearrange("(p t) u -> p t u", t=PACK))
+        nc.sync.dma_start(key_word_pool[:], keys_words[0].rearrange("p c r -> p (c r)").bitcast(I32))
+        nc.sync.dma_start(places[:], offs2)
+        nc.sync.dma_start(q_raw[:], query.rearrange("(p t) q -> p t q", t=PACK))
+        nc.sync.dma_start(size_cols[:], size.rearrange("o (p t) -> (o p) t", t=PACK))
+        for j in range(E // P):
+            nc.sync.dma_start(val_pool[j][:], vals[j * P : (j + 1) * P, :])
+
+        warm = sb.tile([P, 1], F32, name="warm")
+        nc.scalar.activation(warm[:], b_sb[:, U : U + 1], ACT.Exp)
+
+        ident = sb.tile([P, P], F32, name="ident")
+        make_identity(nc, ident[:])
+
+        key_scales = sb.tile([P, I], U8, name="key_scales", align_bytes=64)
+        nc.vector.tensor_copy(key_scales[:], key_scale_pool[:].indirect(slots[:]))
+
+        pq_grouped = sb.tile([P, Q, PACK], BF16, name="pq_grouped", align_bytes=64)
+        interleave(nc.scalar.copy, pq_grouped, pq_raw, 0, Q)
+        pq_codes, pq_scales = quantize(nc, sb, pq_grouped[:].rearrange("p c t -> p (c t)"), Q, "pq")
+
+        place_grouped = sb.tile([P, U, PACK], BF16, name="place_grouped", align_bytes=64)
+        interleave(nc.vector.tensor_copy, place_grouped, place_raw, 0, PLACE_ON_VECTOR)
+        interleave(nc.scalar.copy, place_grouped, place_raw, PLACE_ON_VECTOR, U)
+        place_codes, place_scales = quantize(nc, sb, place_grouped[:].rearrange("p c t -> p (c t)"), U, "place")
+
+        b_ps = ps.tile([P, U], F32, name="b_ps")
+        nc.tensor.matmul_mx(
+            b_ps[:], lhsT=pq_codes[:].bitcast(FP8X4), lhsT_scale=pq_scales[:],
+            rhs=place_codes[:].bitcast(FP8X4), rhs_scale=place_scales[:], start=True, stop=True,
+        )
+        nc.scalar.copy(b_sb[:, :U], b_ps[:])
+
+        key_words = sb.tile([P, I], U32, name="key_words", align_bytes=64)
+        nc.vector.tensor_copy(key_words[:], key_word_pool[:].bitcast(U32).indirect(slots[:]))
+
+        q_grouped = sb.tile([P, Q, PACK], BF16, name="q_grouped", align_bytes=64)
+        interleave(nc.scalar.copy, q_grouped, q_raw, 0, Q)
+        q_codes, q_scales = quantize(nc, sb, q_grouped[:].rearrange("p c t -> p (c t)"), Q, "q")
+        a_ps = ps.tile([P, I], F32, name="a_ps")
+        nc.tensor.matmul_mx(
+            a_ps[:], lhsT=q_codes[:].bitcast(FP8X4), lhsT_scale=q_scales[:],
+            rhs=key_words[:].bitcast(FP8X4), rhs_scale=key_scales[:], start=True, stop=True,
+        )
+
+        size_ps = ps.tile([P, PACK, P], F32, name="size_ps")
+        for t in range(PACK):
+            nc.tensor.transpose(size_ps[:, t, :], size_cols[:, t : t + 1].to_broadcast([P, P]), ident[:])
+
+        b_listed = sb.tile([P, I], F32, name="b_listed")
+        nc.vector.tensor_copy(b_listed[:], b_sb[:].indirect(places[:]))
+
+        def turn(rows, bank, name):
+            words = rows[:].bitcast(F32)
+            for h in range(2):
+                nc.tensor.transpose(bank[:, h, :], words[:, h::2], ident[:])
+            grouped = sb.tile([P, P * PACK], BF16, name=name, align_bytes=64)
+            nc.scalar.copy(
+                grouped[:].bitcast(F32).rearrange("p (c h) -> p c h", h=2), bank[:].rearrange("p h c -> p c h")
+            )
+            return grouped
+
+        def gather_values(j):
+            listed = sb.tile([P, I], BF16, name="v_listed%d" % j, align_bytes=64)
+            nc.vector.tensor_copy(listed[:], val_pool[j][:].indirect(slots[:]))
+            bank = ps2.tile([P, 2, P], F32, name="v_ps")
+            return turn(listed, bank, "v_grouped%d" % j)
+
+        def finish(j, v_codes, v_scales):
+            o_ps = ps2.tile([P, P], F32, name="o_ps")
+            nc.tensor.matmul_mx(
+                o_ps[:], lhsT=w_codes[:].bitcast(FP8X4), lhsT_scale=w_scales[:],
+                rhs=v_codes[:].bitcast(FP8X4), rhs_scale=v_scales[:], start=True, stop=True,
+            )
+            o_sb = sb.tile([P, P], F32, name="o_sb%d" % j)
+            nc.scalar.copy(o_sb[:], o_ps[:])
+            nc.sync.dma_start(out[:, j * P : (j + 1) * P], o_sb[:])
+
+        v0 = gather_values(0)
+        s = sb.tile([P, I], F32, name="s")
+        nc.vector.scalar_tensor_tensor(s[:], b_listed[:], 1.0, a_ps[:], ALU.add, ALU.mult)
+        neg_max = sb.tile([P, 1], F32, name="neg_max")
+        nc.vector.tensor_reduce(neg_max[:], s[:], mybir.AxisListType.X, ALU.max, negate=True)
+        p_sb = sb.tile([P, I], F32, name="p_sb")
+        row_sum = sb.tile([P, 1], F32, name="row_sum")
+        nc.scalar.activation(p_sb[:], s[:], ACT.Exp, bias=neg_max[:], accum_out=row_sum[:])
+        v1 = gather_values(1)
+        inv_sum = sb.tile([P, 1], F32, name="inv_sum")
+        nc.vector.reciprocal(inv_sum[:], row_sum[:])
+        vq0 = quantize(nc, sb, v0[:], P, "v0")
+        w = sb.tile([P, I], BF16, name="w", align_bytes=64)
+        nc.vector.scalar_tensor_tensor(
+            w[:].rearrange("q (s t) -> q s t", t=PACK), p_sb[:].rearrange("q (s t) -> q s t", t=PACK), inv_sum[:],
+            size_ps[:].rearrange("q t s -> q s t"), ALU.mult, ALU.mult,
+        )
+        w_ps = ps.tile([P, 2, P], F32, name="w_ps")
+        w_grouped = turn(w, w_ps, "w_grouped")
+        vq1 = quantize(nc, sb, v1[:], P, "v1")
+        v2 = gather_values(2)
+        w_codes, w_scales = quantize(nc, sb, w_grouped[:], Q, "w")
+        finish(0, *vq0)
+        finish(1, *vq1)
+        finish(2, *quantize(nc, sb, v2[:], P, "v2"))
+        v3 = gather_values(3)
+        finish(3, *quantize(nc, sb, v3[:], P, "v3"))

@@ -29,8 +29,8 @@ def interleave(copy, grouped, raw, c0, c1):
     )
 
 
-def quantize(nc, pool, grouped, width, name):
-    codes = pool.tile([P, width], U32, name=name + "_codes", align_bytes=64)
+def quantize(nc, pool, grouped, width, name, tag=""):
+    codes = pool.tile([P, width], U32, name=name + "_codes", tag=tag, align_bytes=64)
     scales = pool.tile([P, width], U8, name=name + "_scales", align_bytes=64)
     nc.vector.quantize_mx(out=codes[:].bitcast(FP8X4), scales=scales[:], in_=grouped)
     return codes, scales
@@ -43,50 +43,76 @@ def tile_attend_productscores_kernel(tc, query, keys_words, keys_scales, pquery,
         ps = ctx.enter_context(tc.psum_pool(name="ps", bufs=1))
         ps2 = ctx.enter_context(tc.psum_pool(name="ps2", bufs=2))
 
-        slots = sb.tile([P, I // 16], U16, name="slots")
-        places = sb.tile([P, I // 16], U16, name="places")
+        slots = sb.tile([P, I // 16], U16, name="slots", align_bytes=64)
+        places = sb.tile([P, I // 16], U16, name="places", align_bytes=64)
         key_scale_pool = sb.tile([P, T], U8, name="key_scale_pool", align_bytes=64)
         key_word_pool = sb.tile([P, T], I32, name="key_word_pool", align_bytes=64)
-        q_raw = sb.tile([P, PACK, Q], F32, name="q_raw")
-        pq_raw = sb.tile([P, PACK, Q], F32, name="pq_raw")
-        place_raw = sb.tile([P, PACK, U], F32, name="place_raw")
-        size_cols = sb.tile([P, PACK], F32, name="size_cols")
-        val_pool = [sb.tile([P, T], F32, name="val_pool%d" % j) for j in range(E // P)]
-        b_sb = sb.tile([P, B_WINDOW], F32, name="b_sb")
+        q_raw = sb.tile([P, PACK, Q], F32, name="q_raw", align_bytes=64)
+        pq_raw = sb.tile([P, PACK, Q], F32, name="pq_raw", align_bytes=64)
+        place_raw = sb.tile([P, PACK, U], F32, name="place_raw", align_bytes=64)
+        size_cols = sb.tile([P, PACK], F32, name="size_cols", align_bytes=64)
+        val_pool = [sb.tile([P, T], F32, name="val_pool%d" % j, align_bytes=64) for j in range(E // P)]
+        b_sb = sb.tile([P, B_WINDOW], F32, name="b_sb", align_bytes=64)
 
         nc.vector.memset(key_scale_pool[:].bitcast(I32), 0)
-        nc.vector.memset(b_sb[:, U:], 0.0)
+        nc.gpsimd.memset(b_sb[:, U:], 0.0)
+        nc.sync.dma_start(place_raw[:], place.rearrange("(p t) u -> p t u", t=PACK))
         nc.sync.dma_start(slots[:], offs)
+        nc.sync.dma_start(pq_raw[:], pquery.rearrange("(p t) q -> p t q", t=PACK))
         for g in range(4):
-            nc.scalar.dma_start(
+            nc.sync.dma_start(
                 key_scale_pool[32 * g : 32 * g + 4, :].bitcast(I32), keys_scales[0, 4 * g : 4 * g + 4, :].bitcast(I32)
             )
-        nc.sync.dma_start(pq_raw[:], pquery.rearrange("(p t) q -> p t q", t=PACK))
-        nc.sync.dma_start(place_raw[:], place.rearrange("(p t) u -> p t u", t=PACK))
         nc.sync.dma_start(key_word_pool[:], keys_words[0].rearrange("p c r -> p (c r)").bitcast(I32))
-        nc.sync.dma_start(places[:], offs2)
         nc.sync.dma_start(q_raw[:], query.rearrange("(p t) q -> p t q", t=PACK))
+        nc.sync.dma_start(places[:], offs2)
+        nc.sync.dma_start(val_pool[0][:], vals[0:P, :])
         nc.sync.dma_start(size_cols[:], size.rearrange("o (p t) -> (o p) t", t=PACK))
-        for j in range(E // P):
+        for j in range(1, E // P):
             nc.sync.dma_start(val_pool[j][:], vals[j * P : (j + 1) * P, :])
 
-        warm = sb.tile([P, 1], F32, name="warm")
+        warm = sb.tile([P, 1], F32, name="warm", align_bytes=64)
         nc.scalar.activation(warm[:], b_sb[:, U : U + 1], ACT.Exp)
 
-        ident = sb.tile([P, P], F32, name="ident")
+        ident = sb.tile([P, P], F32, name="ident", align_bytes=64)
         make_identity(nc, ident[:])
 
-        key_scales = sb.tile([P, I], U8, name="key_scales", align_bytes=64)
-        nc.vector.tensor_copy(key_scales[:], key_scale_pool[:].indirect(slots[:]))
+        size_ps = ps.tile([P, PACK, P], F32, name="size_ps")
+        w_ps = ps.tile([P, 2, P], F32, name="w_ps")
 
-        pq_grouped = sb.tile([P, Q, PACK], BF16, name="pq_grouped", align_bytes=64)
-        interleave(nc.scalar.copy, pq_grouped, pq_raw, 0, Q)
-        pq_codes, pq_scales = quantize(nc, sb, pq_grouped[:].rearrange("p c t -> p (c t)"), Q, "pq")
+        def turn(rows, bank, grouped):
+            words = rows[:].bitcast(F32)
+            for h in range(2):
+                nc.tensor.transpose(bank[:, h, :], words[:, h::2], ident[:])
+            nc.scalar.copy(
+                grouped.bitcast(F32).rearrange("p (c h) -> p c h", h=2), bank[:].rearrange("p h c -> p c h")
+            )
+
+        def gather_values(j, grouped):
+            listed = sb.tile([P, I], BF16, name="v_listed%d" % j, align_bytes=64)
+            nc.vector.tensor_copy(listed[:], val_pool[j][:].indirect(slots[:]))
+            bank = ps2.tile([P, 2, P], F32, name="v_ps")
+            turn(listed, bank, grouped)
+
+        def finish(e0, v_codes, v_scales):
+            width = v_codes.shape[1]
+            o_ps = ps2.tile([P, width], F32, name="o_ps")
+            nc.tensor.matmul_mx(
+                o_ps[:], lhsT=w_codes.bitcast(FP8X4), lhsT_scale=w_scales[:],
+                rhs=v_codes.bitcast(FP8X4), rhs_scale=v_scales, start=True, stop=True,
+            )
+            o_sb = sb.tile([P, width], F32, name="o_sb%d" % e0, align_bytes=64)
+            nc.scalar.copy(o_sb[:], o_ps[:])
+            nc.sync.dma_start(out[:, e0 : e0 + width], o_sb[:])
 
         place_grouped = sb.tile([P, U, PACK], BF16, name="place_grouped", align_bytes=64)
         interleave(nc.vector.tensor_copy, place_grouped, place_raw, 0, PLACE_ON_VECTOR)
         interleave(nc.scalar.copy, place_grouped, place_raw, PLACE_ON_VECTOR, U)
         place_codes, place_scales = quantize(nc, sb, place_grouped[:].rearrange("p c t -> p (c t)"), U, "place")
+
+        pq_grouped = sb.tile([P, Q, PACK], BF16, name="pq_grouped", tag="place_raw", align_bytes=64)
+        interleave(nc.scalar.copy, pq_grouped, pq_raw, 0, Q)
+        pq_codes, pq_scales = quantize(nc, sb, pq_grouped[:].rearrange("p c t -> p (c t)"), Q, "pq")
 
         b_ps = ps.tile([P, U], F32, name="b_ps")
         nc.tensor.matmul_mx(
@@ -94,76 +120,62 @@ def tile_attend_productscores_kernel(tc, query, keys_words, keys_scales, pquery,
             rhs=place_codes[:].bitcast(FP8X4), rhs_scale=place_scales[:], start=True, stop=True,
         )
         nc.scalar.copy(b_sb[:, :U], b_ps[:])
+        q_grouped = sb.tile([P, Q, PACK], BF16, name="q_grouped", tag="place_codes", align_bytes=64)
+        interleave(nc.scalar.copy, q_grouped, q_raw, 0, Q)
 
+        key_scales = sb.tile([P, I], U8, name="key_scales", tag="place_grouped", align_bytes=64)
+        nc.vector.tensor_copy(key_scales[:], key_scale_pool[:].indirect(slots[:]))
         key_words = sb.tile([P, I], U32, name="key_words", align_bytes=64)
         nc.vector.tensor_copy(key_words[:], key_word_pool[:].bitcast(U32).indirect(slots[:]))
-
-        q_grouped = sb.tile([P, Q, PACK], BF16, name="q_grouped", align_bytes=64)
-        interleave(nc.scalar.copy, q_grouped, q_raw, 0, Q)
-        q_codes, q_scales = quantize(nc, sb, q_grouped[:].rearrange("p c t -> p (c t)"), Q, "q")
+        q_codes, q_scales = quantize(nc, sb, q_grouped[:].rearrange("p c t -> p (c t)"), Q, "q", "key_word_pool")
+        b_listed = sb.tile([P, I], F32, name="b_listed", tag="place_codes", align_bytes=64)
+        nc.vector.tensor_copy(b_listed[:], b_sb[:].indirect(places[:]))
         a_ps = ps.tile([P, I], F32, name="a_ps")
         nc.tensor.matmul_mx(
             a_ps[:], lhsT=q_codes[:].bitcast(FP8X4), lhsT_scale=q_scales[:],
             rhs=key_words[:].bitcast(FP8X4), rhs_scale=key_scales[:], start=True, stop=True,
         )
-
-        size_ps = ps.tile([P, PACK, P], F32, name="size_ps")
         for t in range(PACK):
             nc.tensor.transpose(size_ps[:, t, :], size_cols[:, t : t + 1].to_broadcast([P, P]), ident[:])
 
-        b_listed = sb.tile([P, I], F32, name="b_listed")
-        nc.vector.tensor_copy(b_listed[:], b_sb[:].indirect(places[:]))
+        v2 = sb.tile([P, I], BF16, name="v2_grouped", align_bytes=64)
+        v3 = sb.tile([P, I], BF16, name="v3_grouped", align_bytes=64)
 
-        def turn(rows, bank, name):
-            words = rows[:].bitcast(F32)
-            for h in range(2):
-                nc.tensor.transpose(bank[:, h, :], words[:, h::2], ident[:])
-            grouped = sb.tile([P, P * PACK], BF16, name=name, align_bytes=64)
-            nc.scalar.copy(
-                grouped[:].bitcast(F32).rearrange("p (c h) -> p c h", h=2), bank[:].rearrange("p h c -> p c h")
-            )
-            return grouped
-
-        def gather_values(j):
-            listed = sb.tile([P, I], BF16, name="v_listed%d" % j, align_bytes=64)
-            nc.vector.tensor_copy(listed[:], val_pool[j][:].indirect(slots[:]))
-            bank = ps2.tile([P, 2, P], F32, name="v_ps")
-            return turn(listed, bank, "v_grouped%d" % j)
-
-        def finish(j, v_codes, v_scales):
-            o_ps = ps2.tile([P, P], F32, name="o_ps")
-            nc.tensor.matmul_mx(
-                o_ps[:], lhsT=w_codes[:].bitcast(FP8X4), lhsT_scale=w_scales[:],
-                rhs=v_codes[:].bitcast(FP8X4), rhs_scale=v_scales[:], start=True, stop=True,
-            )
-            o_sb = sb.tile([P, P], F32, name="o_sb%d" % j)
-            nc.scalar.copy(o_sb[:], o_ps[:])
-            nc.sync.dma_start(out[:, j * P : (j + 1) * P], o_sb[:])
-
-        v0 = gather_values(0)
-        s = sb.tile([P, I], F32, name="s")
+        s = sb.tile([P, I], F32, name="s", align_bytes=64)
         nc.vector.scalar_tensor_tensor(s[:], b_listed[:], 1.0, a_ps[:], ALU.add, ALU.mult)
-        neg_max = sb.tile([P, 1], F32, name="neg_max")
+        neg_max = sb.tile([P, 1], F32, name="neg_max", align_bytes=64)
         nc.vector.tensor_reduce(neg_max[:], s[:], mybir.AxisListType.X, ALU.max, negate=True)
-        p_sb = sb.tile([P, I], F32, name="p_sb")
-        row_sum = sb.tile([P, 1], F32, name="row_sum")
+        val0_bf = sb.tile([P, T], BF16, name="val0_bf", align_bytes=64)
+        nc.scalar.activation(val0_bf[:], val_pool[0][:], ACT.Copy)
+        p_sb = sb.tile([P, I], F32, name="p_sb", tag="val_pool0", align_bytes=64)
+        row_sum = sb.tile([P, 1], F32, name="row_sum", align_bytes=64)
         nc.scalar.activation(p_sb[:], s[:], ACT.Exp, bias=neg_max[:], accum_out=row_sum[:])
-        v1 = gather_values(1)
-        inv_sum = sb.tile([P, 1], F32, name="inv_sum")
+        listed0 = sb.tile([P, I], BF16, name="v_listed0", align_bytes=64)
+        nc.scalar.activation(listed0[:], val0_bf[:].indirect(slots[:]), ACT.Copy)
+        grouped = sb.tile([P, 3 * I], BF16, name="grouped", tag="val0_bf", align_bytes=64)
+        v01 = grouped[:, : 2 * I]
+        w_grouped = grouped[:, 2 * I :]
+        gather_values(1, v01[:, I:])
+        inv_sum = sb.tile([P, 1], F32, name="inv_sum", tag="val_pool1", align_bytes=64)
         nc.vector.reciprocal(inv_sum[:], row_sum[:])
-        vq0 = quantize(nc, sb, v0[:], P, "v0")
         w = sb.tile([P, I], BF16, name="w", align_bytes=64)
         nc.vector.scalar_tensor_tensor(
             w[:].rearrange("q (s t) -> q s t", t=PACK), p_sb[:].rearrange("q (s t) -> q s t", t=PACK), inv_sum[:],
             size_ps[:].rearrange("q t s -> q s t"), ALU.mult, ALU.mult,
         )
-        w_ps = ps.tile([P, 2, P], F32, name="w_ps")
-        w_grouped = turn(w, w_ps, "w_grouped")
-        vq1 = quantize(nc, sb, v1[:], P, "v1")
-        v2 = gather_values(2)
-        w_codes, w_scales = quantize(nc, sb, w_grouped[:], Q, "w")
-        finish(0, *vq0)
-        finish(1, *vq1)
-        finish(2, *quantize(nc, sb, v2[:], P, "v2"))
-        v3 = gather_values(3)
-        finish(3, *quantize(nc, sb, v3[:], P, "v3"))
+        turn(w, w_ps, w_grouped)
+        bank0 = ps2.tile([P, 2, P], F32, name="v_ps")
+        turn(listed0, bank0, v01[:, :I])
+        gather_values(2, v2[:])
+        codes = sb.tile([P, 3 * P], U32, name="codes", tag="val_pool2", align_bytes=64)
+        v01_scales = sb.tile([P, 2 * P], U8, name="v01_scales", align_bytes=64)
+        w_scales = sb.tile([P, P], U8, name="w_scales", align_bytes=64)
+        w_codes = codes[:, 2 * P :]
+        nc.vector.quantize_mx(out=w_codes.bitcast(FP8X4), scales=w_scales[:], in_=w_grouped)
+        nc.vector.quantize_mx(out=codes[:, : 2 * P].bitcast(FP8X4), scales=v01_scales[:], in_=v01)
+        finish(0, codes[:, : 2 * P], v01_scales[:])
+        gather_values(3, v3[:])
+        v2_codes, v2_scales = quantize(nc, sb, v2[:], P, "v2", "val_pool3")
+        finish(2 * P, v2_codes[:], v2_scales[:])
+        v3_codes, v3_scales = quantize(nc, sb, v3[:], P, "v3")
+        finish(3 * P, v3_codes[:], v3_scales[:])

@@ -59,10 +59,8 @@ def tile_attend_productscores_kernel(tc, query, keys_words, keys_scales, pquery,
         nc.sync.dma_start(place_raw[:], place.rearrange("(p t) u -> p t u", t=PACK))
         nc.sync.dma_start(slots[:], offs)
         nc.sync.dma_start(pq_raw[:], pquery.rearrange("(p t) q -> p t q", t=PACK))
-        for g in range(4):
-            nc.sync.dma_start(
-                key_scale_pool[32 * g : 32 * g + 4, :].bitcast(I32), keys_scales[0, 4 * g : 4 * g + 4, :].bitcast(I32)
-            )
+        for r in range(4):
+            nc.sync.dma_start(key_scale_pool[r:P:32, :].bitcast(I32), keys_scales[0, r:16:4, :].bitcast(I32))
         nc.sync.dma_start(key_word_pool[:], keys_words[0].rearrange("p c r -> p (c r)").bitcast(I32))
         nc.sync.dma_start(q_raw[:], query.rearrange("(p t) q -> p t q", t=PACK))
         nc.sync.dma_start(places[:], offs2)
@@ -94,15 +92,15 @@ def tile_attend_productscores_kernel(tc, query, keys_words, keys_scales, pquery,
             bank = ps2.tile([P, 2, P], F32, name="v_ps")
             turn(listed, bank, grouped)
 
-        def finish(e0, v_codes, v_scales):
+        def finish(e0, v_codes, v_scales, bank, copy):
             width = v_codes.shape[1]
-            o_ps = ps2.tile([P, width], F32, name="o_ps")
+            o_ps = ps.tile([P, width], F32, name="o_ps%d" % e0, tag=bank)
             nc.tensor.matmul_mx(
-                o_ps[:], lhsT=w_codes.bitcast(FP8X4), lhsT_scale=w_scales[:],
+                o_ps[:], lhsT=w_codes.bitcast(FP8X4), lhsT_scale=w_scales,
                 rhs=v_codes.bitcast(FP8X4), rhs_scale=v_scales, start=True, stop=True,
             )
             o_sb = sb.tile([P, width], F32, name="o_sb%d" % e0, align_bytes=64)
-            nc.scalar.copy(o_sb[:], o_ps[:])
+            copy(o_sb[:], o_ps[:])
             nc.sync.dma_start(out[:, e0 : e0 + width], o_sb[:])
 
         place_grouped = sb.tile([P, U, PACK], BF16, name="place_grouped", align_bytes=64)
@@ -138,7 +136,6 @@ def tile_attend_productscores_kernel(tc, query, keys_words, keys_scales, pquery,
         for t in range(PACK):
             nc.tensor.transpose(size_ps[:, t, :], size_cols[:, t : t + 1].to_broadcast([P, P]), ident[:])
 
-        v2 = sb.tile([P, I], BF16, name="v2_grouped", align_bytes=64)
         v3 = sb.tile([P, I], BF16, name="v3_grouped", align_bytes=64)
 
         s = sb.tile([P, I], F32, name="s", align_bytes=64)
@@ -152,9 +149,10 @@ def tile_attend_productscores_kernel(tc, query, keys_words, keys_scales, pquery,
         nc.scalar.activation(p_sb[:], s[:], ACT.Exp, bias=neg_max[:], accum_out=row_sum[:])
         listed0 = sb.tile([P, I], BF16, name="v_listed0", align_bytes=64)
         nc.scalar.activation(listed0[:], val0_bf[:].indirect(slots[:]), ACT.Copy)
-        grouped = sb.tile([P, 3 * I], BF16, name="grouped", tag="val0_bf", align_bytes=64)
-        v01 = grouped[:, : 2 * I]
-        w_grouped = grouped[:, 2 * I :]
+        grouped = sb.tile([P, 4 * I], BF16, name="grouped", tag="val0_bf", align_bytes=64)
+        w_grouped = grouped[:, :I]
+        v01 = grouped[:, I : 3 * I]
+        v2 = grouped[:, 3 * I :]
         gather_values(1, v01[:, I:])
         inv_sum = sb.tile([P, 1], F32, name="inv_sum", tag="val_pool1", align_bytes=64)
         nc.vector.reciprocal(inv_sum[:], row_sum[:])
@@ -166,16 +164,18 @@ def tile_attend_productscores_kernel(tc, query, keys_words, keys_scales, pquery,
         turn(w, w_ps, w_grouped)
         bank0 = ps2.tile([P, 2, P], F32, name="v_ps")
         turn(listed0, bank0, v01[:, :I])
-        gather_values(2, v2[:])
-        codes = sb.tile([P, 3 * P], U32, name="codes", tag="val_pool2", align_bytes=64)
-        v01_scales = sb.tile([P, 2 * P], U8, name="v01_scales", align_bytes=64)
-        w_scales = sb.tile([P, P], U8, name="w_scales", align_bytes=64)
-        w_codes = codes[:, 2 * P :]
-        nc.vector.quantize_mx(out=w_codes.bitcast(FP8X4), scales=w_scales[:], in_=w_grouped)
-        nc.vector.quantize_mx(out=codes[:, : 2 * P].bitcast(FP8X4), scales=v01_scales[:], in_=v01)
-        finish(0, codes[:, : 2 * P], v01_scales[:])
+        gather_values(2, v2)
         gather_values(3, v3[:])
-        v2_codes, v2_scales = quantize(nc, sb, v2[:], P, "v2", "val_pool3")
-        finish(2 * P, v2_codes[:], v2_scales[:])
+        codes = sb.tile([P, 4 * P], U32, name="codes", tag="val_pool3", align_bytes=64)
+        scales = sb.tile([P, 4 * P], U8, name="scales", align_bytes=64)
+        for half in range(2):
+            cols = slice(2 * P * half, 2 * P * (half + 1))
+            nc.vector.quantize_mx(
+                out=codes[:, cols].bitcast(FP8X4), scales=scales[:, cols], in_=grouped[:, 2 * I * half : 2 * I * (half + 1)]
+            )
+        w_codes = codes[:, :P]
+        w_scales = scales[:, :P]
+        finish(0, codes[:, P : 2 * P], scales[:, P : 2 * P], "b_ps", nc.scalar.copy)
+        finish(P, codes[:, 2 * P :], scales[:, 2 * P :], "a_ps", nc.scalar.copy)
         v3_codes, v3_scales = quantize(nc, sb, v3[:], P, "v3")
-        finish(3 * P, v3_codes[:], v3_scales[:])
+        finish(3 * P, v3_codes[:], v3_scales[:], "size_ps", nc.vector.tensor_copy)

from contextlib import ExitStack

import concourse.mybir as mybir
from concourse.masks import make_identity

D, T, I, Q, E, U = 512, 2048, 512, 128, 512, 512
FLOPS = 2 * Q * D * I + 2 * Q * D * U + 2 * Q * I * E

F32 = mybir.dt.float32
BF16 = mybir.dt.bfloat16
I32 = mybir.dt.int32
U32 = mybir.dt.uint32
U16 = mybir.dt.uint16
U8 = mybir.dt.uint8
FP8X4 = mybir.dt.float8_e4m3fn_x4
ALU = mybir.AluOpType
ACT = mybir.ActivationFunctionType

P = 128
PACK = 4
B_WINDOW = U + 192
PLACE_ON_VECTOR = 320


def interleave(copy, grouped, raw, c0, c1):
    copy(
        out=grouped[:, c0:c1, :].rearrange("p (c i) t -> p c t i", i=4),
        in_=raw[:, :, c0:c1].rearrange("p t (c i) -> p c t i", i=4),
    )


def quantize(nc, pool, grouped, width, name, tag=""):
    codes = pool.tile([P, width], U32, name=name + "_codes", tag=tag, align_bytes=64)
    scales = pool.tile([P, width], U8, name=name + "_scales", align_bytes=64)
    nc.vector.quantize_mx(out=codes[:].bitcast(FP8X4), scales=scales[:], in_=grouped)
    return codes, scales


def tile_attend_productscores_kernel(tc, query, keys_words, keys_scales, pquery, place, size, vals, offs, offs2, out):
    nc = tc.nc
    with ExitStack() as ctx:
        sb = ctx.enter_context(tc.tile_pool(name="sb", bufs=1))
        ps = ctx.enter_context(tc.psum_pool(name="ps", bufs=1))
        ps2 = ctx.enter_context(tc.psum_pool(name="ps2", bufs=2))

        slots = sb.tile([P, I // 16], U16, name="slots", align_bytes=64)
        places = sb.tile([P, I // 16], U16, name="places", align_bytes=64)
        key_scale_pool = sb.tile([P, T], U8, name="key_scale_pool", align_bytes=64)
        key_word_pool = sb.tile([P, T], I32, name="key_word_pool", align_bytes=64)
        q_raw = sb.tile([P, PACK, Q], F32, name="q_raw", align_bytes=64)
        pq_raw = sb.tile([P, PACK, Q], F32, name="pq_raw", align_bytes=64)
        place_raw = sb.tile([P, PACK, U], F32, name="place_raw", align_bytes=64)
        size_cols = sb.tile([P, PACK], F32, name="size_cols", align_bytes=64)
        val_pool = [sb.tile([P, T], F32, name="val_pool%d" % j, align_bytes=64) for j in range(E // P)]
        b_sb = sb.tile([P, B_WINDOW], F32, name="b_sb", align_bytes=64)

        nc.vector.memset(key_scale_pool[:].bitcast(I32), 0)
        nc.gpsimd.memset(b_sb[:, U:], 0.0)
        nc.sync.dma_start(place_raw[:], place.rearrange("(p t) u -> p t u", t=PACK))
        nc.sync.dma_start(slots[:], offs)
        nc.sync.dma_start(pq_raw[:], pquery.rearrange("(p t) q -> p t q", t=PACK))
        for r in range(4):
            nc.sync.dma_start(key_scale_pool[r:P:32, :].bitcast(I32), keys_scales[0, r:16:4, :].bitcast(I32))
        nc.sync.dma_start(key_word_pool[:], keys_words[0].rearrange("p c r -> p (c r)").bitcast(I32))
        nc.sync.dma_start(q_raw[:], query.rearrange("(p t) q -> p t q", t=PACK))
        nc.sync.dma_start(places[:], offs2)
        nc.sync.dma_start(val_pool[0][:], vals[0:P, :])
        nc.sync.dma_start(size_cols[:], size.rearrange("o (p t) -> (o p) t", t=PACK))
        for j in range(1, E // P):
            nc.sync.dma_start(val_pool[j][:], vals[j * P : (j + 1) * P, :])

        warm = sb.tile([P, 1], F32, name="warm", align_bytes=64)
        nc.scalar.activation(warm[:], b_sb[:, U : U + 1], ACT.Exp)

        ident = sb.tile([P, P], F32, name="ident", align_bytes=64)
        make_identity(nc, ident[:])

        size_ps = ps.tile([P, PACK, P], F32, name="size_ps")
        w_ps = ps.tile([P, 2, P], F32, name="w_ps")

        def turn(rows, bank, grouped):
            words = rows[:].bitcast(F32)
            for h in range(2):
                nc.tensor.transpose(bank[:, h, :], words[:, h::2], ident[:])
            nc.scalar.copy(
                grouped.bitcast(F32).rearrange("p (c h) -> p c h", h=2), bank[:].rearrange("p h c -> p c h")
            )

        def gather_values(j, grouped):
            listed = sb.tile([P, I], BF16, name="v_listed%d" % j, align_bytes=64)
            nc.vector.tensor_copy(listed[:], val_pool[j][:].indirect(slots[:]))
            bank = ps2.tile([P, 2, P], F32, name="v_ps")
            turn(listed, bank, grouped)

        def finish(e0, v_codes, v_scales, bank, copy):
            width = v_codes.shape[1]
            o_ps = ps.tile([P, width], F32, name="o_ps%d" % e0, tag=bank)
            nc.tensor.matmul_mx(
                o_ps[:], lhsT=w_codes.bitcast(FP8X4), lhsT_scale=w_scales,
                rhs=v_codes.bitcast(FP8X4), rhs_scale=v_scales, start=True, stop=True,
            )
            o_sb = sb.tile([P, width], F32, name="o_sb%d" % e0, align_bytes=64)
            copy(o_sb[:], o_ps[:])
            nc.sync.dma_start(out[:, e0 : e0 + width], o_sb[:])

        place_grouped = sb.tile([P, U, PACK], BF16, name="place_grouped", align_bytes=64)
        interleave(nc.vector.tensor_copy, place_grouped, place_raw, 0, PLACE_ON_VECTOR)
        interleave(nc.scalar.copy, place_grouped, place_raw, PLACE_ON_VECTOR, U)
        place_codes, place_scales = quantize(nc, sb, place_grouped[:].rearrange("p c t -> p (c t)"), U, "place")

        pq_grouped = sb.tile([P, Q, PACK], BF16, name="pq_grouped", tag="place_raw", align_bytes=64)
        interleave(nc.scalar.copy, pq_grouped, pq_raw, 0, Q)
        pq_codes, pq_scales = quantize(nc, sb, pq_grouped[:].rearrange("p c t -> p (c t)"), Q, "pq")

        b_ps = ps.tile([P, U], F32, name="b_ps")
        nc.tensor.matmul_mx(
            b_ps[:], lhsT=pq_codes[:].bitcast(FP8X4), lhsT_scale=pq_scales[:],
            rhs=place_codes[:].bitcast(FP8X4), rhs_scale=place_scales[:], start=True, stop=True,
        )
        nc.scalar.copy(b_sb[:, :U], b_ps[:])
        q_grouped = sb.tile([P, Q, PACK], BF16, name="q_grouped", tag="place_codes", align_bytes=64)
        interleave(nc.scalar.copy, q_grouped, q_raw, 0, Q)

        key_scales = sb.tile([P, I], U8, name="key_scales", tag="place_grouped", align_bytes=64)
        nc.vector.tensor_copy(key_scales[:], key_scale_pool[:].indirect(slots[:]))
        key_words = sb.tile([P, I], U32, name="key_words", align_bytes=64)
        nc.vector.tensor_copy(key_words[:], key_word_pool[:].bitcast(U32).indirect(slots[:]))
        q_codes, q_scales = quantize(nc, sb, q_grouped[:].rearrange("p c t -> p (c t)"), Q, "q", "key_word_pool")
        b_listed = sb.tile([P, I], F32, name="b_listed", tag="place_codes", align_bytes=64)
        nc.vector.tensor_copy(b_listed[:], b_sb[:].indirect(places[:]))
        a_ps = ps.tile([P, I], F32, name="a_ps")
        nc.tensor.matmul_mx(
            a_ps[:], lhsT=q_codes[:].bitcast(FP8X4), lhsT_scale=q_scales[:],
            rhs=key_words[:].bitcast(FP8X4), rhs_scale=key_scales[:], start=True, stop=True,
        )
        for t in range(PACK):
            nc.tensor.transpose(size_ps[:, t, :], size_cols[:, t : t + 1].to_broadcast([P, P]), ident[:])

        v3 = sb.tile([P, I], BF16, name="v3_grouped", align_bytes=64)

        s = sb.tile([P, I], F32, name="s", align_bytes=64)
        nc.vector.scalar_tensor_tensor(s[:], b_listed[:], 1.0, a_ps[:], ALU.add, ALU.mult)
        neg_max = sb.tile([P, 1], F32, name="neg_max", align_bytes=64)
        nc.vector.tensor_reduce(neg_max[:], s[:], mybir.AxisListType.X, ALU.max, negate=True)
        val0_bf = sb.tile([P, T], BF16, name="val0_bf", align_bytes=64)
        nc.scalar.activation(val0_bf[:], val_pool[0][:], ACT.Copy)
        p_sb = sb.tile([P, I], F32, name="p_sb", tag="val_pool0", align_bytes=64)
        row_sum = sb.tile([P, 1], F32, name="row_sum", align_bytes=64)
        nc.scalar.activation(p_sb[:], s[:], ACT.Exp, bias=neg_max[:], accum_out=row_sum[:])
        listed0 = sb.tile([P, I], BF16, name="v_listed0", align_bytes=64)
        nc.scalar.activation(listed0[:], val0_bf[:].indirect(slots[:]), ACT.Copy)
        grouped = sb.tile([P, 4 * I], BF16, name="grouped", tag="val0_bf", align_bytes=64)
        w_grouped = grouped[:, :I]
        v01 = grouped[:, I : 3 * I]
        v2 = grouped[:, 3 * I :]
        gather_values(1, v01[:, I:])
        inv_sum = sb.tile([P, 1], F32, name="inv_sum", tag="val_pool1", align_bytes=64)
        nc.vector.reciprocal(inv_sum[:], row_sum[:])
        w = sb.tile([P, I], BF16, name="w", align_bytes=64)
        nc.vector.scalar_tensor_tensor(
            w[:].rearrange("q (s t) -> q s t", t=PACK), p_sb[:].rearrange("q (s t) -> q s t", t=PACK), inv_sum[:],
            size_ps[:].rearrange("q t s -> q s t"), ALU.mult, ALU.mult,
        )
        turn(w, w_ps, w_grouped)
        bank0 = ps2.tile([P, 2, P], F32, name="v_ps")
        turn(listed0, bank0, v01[:, :I])
        gather_values(2, v2)
        gather_values(3, v3[:])
        codes = sb.tile([P, 4 * P], U32, name="codes", tag="val_pool3", align_bytes=64)
        scales = sb.tile([P, 4 * P], U8, name="scales", align_bytes=64)
        for half in range(2):
            cols = slice(2 * P * half, 2 * P * (half + 1))
            nc.vector.quantize_mx(
                out=codes[:, cols].bitcast(FP8X4), scales=scales[:, cols], in_=grouped[:, 2 * I * half : 2 * I * (half + 1)]
            )
        w_codes = codes[:, :P]
        w_scales = scales[:, :P]
        finish(0, codes[:, P : 2 * P], scales[:, P : 2 * P], "b_ps", nc.scalar.copy)
        finish(P, codes[:, 2 * P :], scales[:, 2 * P :], "a_ps", nc.scalar.copy)
        v3_codes, v3_scales = quantize(nc, sb, v3[:], P, "v3")
        finish(3 * P, v3_codes[:], v3_scales[:], "size_ps", nc.vector.tensor_copy)
